import numpy as np
import ml_dtypes


def mxq(x, axis, fmt="e4m3"):
    dtype, down = {"e4m3": (ml_dtypes.float8_e4m3fn, 7), "e5m2": (ml_dtypes.float8_e5m2, 14)}[fmt]
    v = np.moveaxis(np.asarray(x, np.float32).astype(ml_dtypes.bfloat16).astype(np.float64), axis, -1)
    blocks = v.reshape(v.shape[:-1] + (-1, 32))
    amax = np.abs(blocks).max(-1, keepdims=True)
    byte = np.maximum(np.where(amax > 0, np.frexp(amax)[1] - 1 + 127, 0) - down, 1)
    scale = np.exp2(byte - 127.0)
    codes = (blocks / scale).astype(np.float32).astype(dtype).astype(np.float64)
    return np.moveaxis((codes * scale).reshape(v.shape), -1, axis)


WIDE = False


def mx_kscale(k):
    if not WIDE:
        return np.ones(k)
    levels = np.array([10, -10, 5, -5, 0])
    if k % 512:
        return np.exp2(np.random.permutation(np.resize(levels, k // 32))).repeat(32)
    a = np.empty((k // 512, 16))
    for p in range(k // 512):
        a[p, :8] = np.random.permutation(np.resize(levels, 8))
        for g in range(8):
            far = levels[np.abs(levels - a[p, g]) >= 10]
            a[p, g + 8] = far[np.random.randint(len(far))]
    return np.exp2(a.ravel()).repeat(32)


def f64(x):
    return np.asarray(x).astype(np.float64)


def striped(idx):
    return np.tile(idx.reshape(-1, 16).T, (8, 1)).astype(np.uint16)


def unstriped(offs):
    return offs[:16].T.reshape(-1).astype(np.int64)


E2M1 = np.array([0.0, 0.5, 1.0, 1.5, 2.0, 3.0, 4.0, 6.0, -0.0, -0.5, -1.0, -1.5, -2.0, -3.0, -4.0, -6.0])


def pack_weight(w, fmt):
    k, n = w.shape
    w = f64(np.asarray(w, np.float32).astype(ml_dtypes.bfloat16)).reshape(k // 32, 32, n)
    amax = np.abs(w).max(1)
    if fmt == "e4m3":
        byte = np.frexp(amax)[1] - 1 + 127 - 7
    else:
        mant, ex = np.frexp(amax / 6.0)
        byte = np.where(mant > 0.5, ex, ex - 1) + 127
    byte = np.clip(np.where(amax > 0, byte, 1), 1, 254)
    scaled = (w * np.exp2(127.0 - byte)[:, None, :]).reshape(k, n).astype(np.float32)
    by_word = np.ascontiguousarray(scaled.reshape(k // 512, 128, 4, n).transpose(0, 1, 3, 2))
    if fmt == "e4m3":
        words = by_word.astype(ml_dtypes.float8_e4m3fn).view(np.uint8)
    else:
        c = by_word.astype(ml_dtypes.float4_e2m1fn).view(np.uint8) & 0xF
        words = (c[..., 0::2] | (c[..., 1::2] << 4)).reshape(k // 512, 128, 2 * n)
    return np.ascontiguousarray(words), np.ascontiguousarray(byte.astype(np.uint8).reshape(k // 512, 16, n))


def unpack_weight(words, scales, fmt):
    g, _, n = scales.shape
    words = np.ascontiguousarray(words).reshape(g, 128, n, -1)
    if fmt == "e4m3":
        vals = words.view(ml_dtypes.float8_e4m3fn).astype(np.float64)
    else:
        nib = np.empty((g, 128, n, 4), np.uint8)
        nib[..., 0::2] = words & 0xF
        nib[..., 1::2] = words >> 4
        vals = E2M1[nib]
    vals = vals * np.repeat(np.exp2(scales.astype(np.float64) - 127.0), 8, axis=1)[..., None]
    return vals.transpose(0, 1, 3, 2).reshape(g * 512, n)


def relu(v):
    return np.maximum(v, 0.0)


K, T, E, C, N = 1024, 1280, 8, 128, 256


def by_expert(wq, xq):
    return np.concatenate([wq[e].T @ xq[:, e * C:(e + 1) * C] for e in range(E)], axis=1)


def setup_inputs():
    n = np.random.standard_normal
    s = mx_kscale(K)[:, None]
    w = [pack_weight(m, "e2m1") for m in n((E, K, N)) / np.sqrt(K) / s[None]]
    return {
        "xT": (n((K, T)) * s).astype(np.float32),
        "w_words": np.stack([m[0] for m in w]),
        "w_scales": np.stack([m[1] for m in w]),
        "b": (0.3 * n((N, E))).astype(np.float32),
        "gate": np.tile(np.random.uniform(0.2, 1.0, E * C), (N, 1)).astype(np.float32),
        "offs": striped(np.random.permutation(T)[:E * C]),
        "dst": striped(np.random.permutation(T)[:E * C]),
    }


def reference(xT, w_words, w_scales, b, gate, offs, dst):
    idx = unstriped(offs)
    w = np.stack([unpack_weight(w_words[e], w_scales[e], "e2m1") for e in range(E)])
    xq = mxq(f64(xT)[:, idx], 0, "e4m3")
    y = by_expert(w, xq)
    y = relu(y + np.repeat(f64(b), C, axis=1))
    out = np.zeros((N, T))
    out[:, unstriped(dst)] = f64(gate) * y
    return out

@@ -1,0 +1,140 @@
+from contextlib import ExitStack
+
+import concourse.mybir as mybir
+
+K, T, E, C, N = 1024, 1280, 8, 128, 256
+SLOTS = E * C
+FLOPS = 2 * K * SLOTS * N
+P = 128
+PACK = 4
+PASSES = K // (P * PACK)
+HALVES = N // P
+
+F32 = mybir.dt.float32
+BF16 = mybir.dt.bfloat16
+I32 = mybir.dt.int32
+U32 = mybir.dt.uint32
+U16 = mybir.dt.uint16
+U8 = mybir.dt.uint8
+FP8X4 = mybir.dt.float8_e4m3fn_x4
+FP4X4 = mybir.dt.float4_e2m1fn_x4
+COPY = mybir.ActivationFunctionType.Copy
+RELU = mybir.ActivationFunctionType.Relu
+MULT = mybir.AluOpType.mult
+
+CHUNKS = {
+    (0, 0): ((0, 384, 224), (384, 512, 288), (896, 384, 224)),
+    (0, 1): ((0, 640, 0), (640, 384, 0), (1024, 256, 128)),
+    (1, 0): ((0, 640, 0), (640, 384, 0), (1024, 256, 0)),
+    (1, 1): ((0, 640, 0), (640, 384, 0), (1024, 256, 128)),
+}
+PIECE = 512
+
+
+def tile_moe_two_lin_relu_kernel(tc, xT, w_words, w_scales, b, gate, offs, dst, out):
+    nc = tc.nc
+    with ExitStack() as ctx:
+        keep = ctx.enter_context(tc.tile_pool(name="keep", bufs=1))
+        psum = ctx.enter_context(tc.psum_pool(name="psum", bufs=1))
+
+        offs_t = keep.tile([P, SLOTS // 16], U16, name="offs_t")
+        dst_t = keep.tile([P, SLOTS // 16], U16, name="dst_t")
+        ww = keep.tile([P, E * PASSES, 2 * N], U8, name="ww", align_bytes=64)
+        ws = keep.tile([P, E * PASSES, N], U8, name="ws", align_bytes=64)
+        gate_t = [keep.tile([P, SLOTS], F32, name=f"gate{h}") for h in range(HALVES)]
+        bias = keep.tile([P, HALVES, E], F32, name="bias")
+        out_t = [keep.tile([P, T], F32, name=f"out{h}") for h in range(HALVES)]
+        pairs = {(a, u): keep.tile([P, T, 2], BF16, name=f"pairs{a}{u}") for a in range(PASSES) for u in range(2)}
+        slots = [keep.tile([P, SLOTS, PACK], BF16, name=f"slots{a}", align_bytes=64) for a in range(PASSES)]
+        codes = [keep.tile([P, SLOTS], U32, name=f"codes{a}", align_bytes=64) for a in range(PASSES)]
+        planes = [keep.tile([P, SLOTS], U8, name=f"planes{a}", align_bytes=64) for a in range(PASSES)]
+
+        nc.gpsimd.memset(ws[:].rearrange("p x n -> p (x n)").bitcast(I32), 0)
+        for h in range(HALVES):
+            nc.gpsimd.memset(out_t[h][:], 0.0)
+
+        x_rows = xT.rearrange("(a p u e) t -> a u p e t", p=P, u=2, e=2)
+        raw = {}
+        for (a, u), chunks in CHUNKS.items():
+            for t0, w, v in chunks:
+                raw[a, u, t0] = keep.tile([P, 2, w], F32, name=f"raw{a}{u}_{t0}")
+                nc.sync.dma_start(raw[a, u, t0][:], x_rows[a, u, :, :, t0 : t0 + w])
+            if (a, u) == (0, 0):
+                nc.sync.dma_start(offs_t[:], offs)
+        s_rows = w_scales.rearrange("e a q n -> q (e a) n")
+        for q in range(4):
+            nc.sync.dma_start(
+                ws[32 * q : 32 * q + 4, :, :].bitcast(I32), s_rows[4 * q : 4 * q + 4, :, :].bitcast(I32)
+            )
+        w_rows = w_words.rearrange("e a p n -> p (e a) n")
+        for part in range(2):
+            x = slice(part * E * PASSES // 2, (part + 1) * E * PASSES // 2)
+            nc.sync.dma_start(ww[:, x, :].bitcast(I32), w_rows[:, x, :].bitcast(I32))
+            if part == 0:
+                nc.sync.dma_start(bias[:], b.rearrange("(h p) e -> p h e", p=P))
+                nc.sync.dma_start(dst_t[:], dst)
+                nc.sync.dma_start(gate_t[0][:], gate[0:P, :])
+        nc.sync.dma_start(gate_t[1][:], gate[P : 2 * P, :])
+
+        def quantise(a, s):
+            nc.vector.quantize_mx(
+                out=codes[a][:, s : s + PIECE].bitcast(FP8X4),
+                scales=planes[a][:, s : s + PIECE],
+                in_=slots[a][:, s : s + PIECE, :].rearrange("p w j -> p (w j)"),
+            )
+
+        for (a, u), chunks in CHUNKS.items():
+            for t0, w, v in chunks:
+                src = raw[a, u, t0][:].rearrange("p e t -> p t e")
+                if v > 0:
+                    nc.vector.tensor_copy(pairs[a, u][:, t0 : t0 + v, :], src[:, 0:v, :])
+                if v < w:
+                    nc.scalar.activation(pairs[a, u][:, t0 + v : t0 + w, :], src[:, v:w, :], COPY)
+            window = pairs[a, u][:].rearrange("p t e -> p (t e)").bitcast(U32)
+            for s in range(0, SLOTS, PIECE):
+                nc.vector.tensor_copy(
+                    slots[a][:, s : s + PIECE, :].bitcast(U32)[:, :, u],
+                    window.indirect(offs_t[:, s // 16 : (s + PIECE) // 16]),
+                )
+                if (a, u) == (1, 1):
+                    quantise(a, s)
+            if (a, u) == (0, 1):
+                for s in range(0, SLOTS, PIECE):
+                    quantise(a, s)
+
+        y = {}
+        per = PIECE // C
+        for s in range(0, SLOTS, PIECE):
+            acc = {}
+            for a in range(PASSES):
+                for h in range(HALVES):
+                    for i in range(per):
+                        if a == 0:
+                            acc[h, i] = psum.tile([P, C], F32, name=f"acc{h}_{i}")
+                        e = s // C + i
+                        x = e * PASSES + a
+                        nc.tensor.matmul_mx(
+                            out=acc[h, i][:],
+                            lhsT=ww[:, x, h * 2 * P : (h + 1) * 2 * P].bitcast(FP4X4),
+                            lhsT_scale=ws[:, x, h * P : (h + 1) * P],
+                            rhs=codes[a][:, e * C : (e + 1) * C].bitcast(FP8X4),
+                            rhs_scale=planes[a][:, e * C : (e + 1) * C],
+                            start=(a == 0),
+                            stop=(a == PASSES - 1),
+                        )
+            for h in range(HALVES):
+                y[h, s] = keep.tile([P, PIECE], F32, name=f"y{h}_{s}")
+                for i in range(per):
+                    e = s // C + i
+                    nc.scalar.activation(
+                        y[h, s][:, i * C : (i + 1) * C], acc[h, i][:], RELU, bias=bias[:, h, e : e + 1]
+                    )
+        for h in range(HALVES):
+            for s in range(0, SLOTS, PIECE):
+                nc.vector.tensor_tensor(
+                    out_t[h][:].indirect(dst_t[:, s // 16 : (s + PIECE) // 16]),
+                    y[h, s][:],
+                    gate_t[h][:, s : s + PIECE],
+                    MULT,
+                )
+            nc.sync.dma_start(out[h * P : (h + 1) * P, :], out_t[h][:])

@@ -22,13 +22,18 @@ COPY = mybir.ActivationFunctionType.Copy
 RELU = mybir.ActivationFunctionType.Relu
 MULT = mybir.AluOpType.mult
 
-CHUNKS = {
-    (0, 0): ((0, 384, 224), (384, 512, 288), (896, 384, 224)),
-    (0, 1): ((0, 640, 0), (640, 384, 0), (1024, 256, 128)),
-    (1, 0): ((0, 640, 0), (640, 384, 0), (1024, 256, 0)),
-    (1, 1): ((0, 640, 0), (640, 384, 0), (1024, 256, 128)),
-}
+CHUNKS = (
+    ((0, 256, 160), (256, 512, 320), (768, 256, 160), (1024, 256, 160)),
+    ((0, 512, 0), (512, 512, 0), (1024, 256, 128)),
+)
 PIECE = 512
+
+
+def interleave(copy, grouped, raw, a, b):
+    copy(
+        grouped[:, a:b, :].rearrange("p (c i) t -> p c t i", i=4),
+        raw[:, :, a:b].rearrange("p t (c i) -> p c t i", i=4),
+    )
 
 
 def tile_moe_two_lin_relu_kernel(tc, xT, w_words, w_scales, b, gate, offs, dst, out):
@@ -44,23 +49,29 @@ def tile_moe_two_lin_relu_kernel(tc, xT, w_words, w_scales, b, gate, offs, dst, 
         gate_t = [keep.tile([P, SLOTS], F32, name=f"gate{h}") for h in range(HALVES)]
         bias = keep.tile([P, HALVES, E], F32, name="bias")
         out_t = [keep.tile([P, T], F32, name=f"out{h}") for h in range(HALVES)]
-        pairs = {(a, u): keep.tile([P, T, 2], BF16, name=f"pairs{a}{u}") for a in range(PASSES) for u in range(2)}
-        slots = [keep.tile([P, SLOTS, PACK], BF16, name=f"slots{a}", align_bytes=64) for a in range(PASSES)]
-        codes = [keep.tile([P, SLOTS], U32, name=f"codes{a}", align_bytes=64) for a in range(PASSES)]
-        planes = [keep.tile([P, SLOTS], U8, name=f"planes{a}", align_bytes=64) for a in range(PASSES)]
+        codes = [keep.tile([P, T], U32, name=f"codes{a}", align_bytes=64) for a in range(PASSES)]
+        planes = [keep.tile([P, T], U8, name=f"planes{a}", align_bytes=64) for a in range(PASSES)]
+        g_codes = [keep.tile([P, SLOTS], U32, name=f"gcodes{a}", align_bytes=64) for a in range(PASSES)]
+        g_planes = [keep.tile([P, SLOTS], U8, name=f"gplanes{a}", align_bytes=64) for a in range(PASSES)]
+        raw = {}
+        grouped = {}
+        for a in range(PASSES):
+            for c, (t0, w, v) in enumerate(CHUNKS[a]):
+                raw[a, c] = keep.tile([P, PACK, w], F32, name=f"raw{a}_{c}")
+                grouped[a, c] = keep.tile([P, w, PACK], BF16, name=f"grouped{a}_{c}", align_bytes=64)
 
+        for a in range(PASSES):
+            nc.gpsimd.memset(planes[a][:].bitcast(I32), 0)
         nc.gpsimd.memset(ws[:].rearrange("p x n -> p (x n)").bitcast(I32), 0)
         for h in range(HALVES):
             nc.gpsimd.memset(out_t[h][:], 0.0)
 
-        x_rows = xT.rearrange("(a p u e) t -> a u p e t", p=P, u=2, e=2)
-        raw = {}
-        for (a, u), chunks in CHUNKS.items():
-            for t0, w, v in chunks:
-                raw[a, u, t0] = keep.tile([P, 2, w], F32, name=f"raw{a}{u}_{t0}")
-                nc.sync.dma_start(raw[a, u, t0][:], x_rows[a, u, :, :, t0 : t0 + w])
-            if (a, u) == (0, 0):
-                nc.sync.dma_start(offs_t[:], offs)
+        x_rows = xT.rearrange("(a p j) t -> a p j t", p=P, j=PACK)
+        for a in range(PASSES):
+            for c, (t0, w, v) in enumerate(CHUNKS[a]):
+                nc.sync.dma_start(raw[a, c][:], x_rows[a, :, :, t0 : t0 + w])
+                if (a, c) == (0, 1):
+                    nc.sync.dma_start(offs_t[:], offs)
         s_rows = w_scales.rearrange("e a q n -> q (e a) n")
         for q in range(4):
             nc.sync.dma_start(
@@ -76,31 +87,23 @@ def tile_moe_two_lin_relu_kernel(tc, xT, w_words, w_scales, b, gate, offs, dst, 
                 nc.sync.dma_start(gate_t[0][:], gate[0:P, :])
         nc.sync.dma_start(gate_t[1][:], gate[P : 2 * P, :])
 
-        def quantise(a, s):
-            nc.vector.quantize_mx(
-                out=codes[a][:, s : s + PIECE].bitcast(FP8X4),
-                scales=planes[a][:, s : s + PIECE],
-                in_=slots[a][:, s : s + PIECE, :].rearrange("p w j -> p (w j)"),
-            )
+        def scalar_copy(o, i):
+            nc.scalar.activation(o, i, COPY)
 
-        for (a, u), chunks in CHUNKS.items():
-            for t0, w, v in chunks:
-                src = raw[a, u, t0][:].rearrange("p e t -> p t e")
+        for a in range(PASSES):
+            for c, (t0, w, v) in enumerate(CHUNKS[a]):
                 if v > 0:
-                    nc.vector.tensor_copy(pairs[a, u][:, t0 : t0 + v, :], src[:, 0:v, :])
-                if v < w:
-                    nc.scalar.activation(pairs[a, u][:, t0 + v : t0 + w, :], src[:, v:w, :], COPY)
-            window = pairs[a, u][:].rearrange("p t e -> p (t e)").bitcast(U32)
-            for s in range(0, SLOTS, PIECE):
-                nc.vector.tensor_copy(
-                    slots[a][:, s : s + PIECE, :].bitcast(U32)[:, :, u],
-                    window.indirect(offs_t[:, s // 16 : (s + PIECE) // 16]),
+                    interleave(nc.vector.tensor_copy, grouped[a, c], raw[a, c], 0, v)
+                interleave(scalar_copy, grouped[a, c], raw[a, c], v, w)
+                nc.vector.quantize_mx(
+                    out=codes[a][:, t0 : t0 + w].bitcast(FP8X4),
+                    scales=planes[a][:, t0 : t0 + w],
+                    in_=grouped[a, c][:].rearrange("p w j -> p (w j)"),
                 )
-                if (a, u) == (1, 1):
-                    quantise(a, s)
-            if (a, u) == (0, 1):
-                for s in range(0, SLOTS, PIECE):
-                    quantise(a, s)
+            for s in range(0, SLOTS, PIECE):
+                lst = offs_t[:, s // 16 : (s + PIECE) // 16]
+                nc.vector.tensor_copy(g_codes[a][:, s : s + PIECE], codes[a][:].indirect(lst))
+                nc.vector.tensor_copy(g_planes[a][:, s : s + PIECE], planes[a][:].indirect(lst))
 
         y = {}
         per = PIECE // C
@@ -117,8 +120,8 @@ def tile_moe_two_lin_relu_kernel(tc, xT, w_words, w_scales, b, gate, offs, dst, 
                             out=acc[h, i][:],
                             lhsT=ww[:, x, h * 2 * P : (h + 1) * 2 * P].bitcast(FP4X4),
                             lhsT_scale=ws[:, x, h * P : (h + 1) * P],
-                            rhs=codes[a][:, e * C : (e + 1) * C].bitcast(FP8X4),
-                            rhs_scale=planes[a][:, e * C : (e + 1) * C],
+                            rhs=g_codes[a][:, e * C : (e + 1) * C].bitcast(FP8X4),
+                            rhs_scale=g_planes[a][:, e * C : (e + 1) * C],
                             start=(a == 0),
                             stop=(a == PASSES - 1),
                         )

@@ -23,8 +23,8 @@ RELU = mybir.ActivationFunctionType.Relu
 MULT = mybir.AluOpType.mult
 
 CHUNKS = (
-    ((0, 256, 160), (256, 512, 320), (768, 256, 160), (1024, 256, 160)),
-    ((0, 512, 0), (512, 512, 0), (1024, 256, 128)),
+    ((0, 256, 160), (256, 512, 336), (768, 256, 192), (1024, 256, 192)),
+    ((0, 512, 0), (512, 512, 64), (1024, 256, 128)),
 )
 PIECE = 512
 
@@ -70,8 +70,8 @@ def tile_moe_two_lin_relu_kernel(tc, xT, w_words, w_scales, b, gate, offs, dst, 
         for a in range(PASSES):
             for c, (t0, w, v) in enumerate(CHUNKS[a]):
                 nc.sync.dma_start(raw[a, c][:], x_rows[a, :, :, t0 : t0 + w])
-                if (a, c) == (0, 1):
-                    nc.sync.dma_start(offs_t[:], offs)
+            if a == 0:
+                nc.sync.dma_start(offs_t[:], offs)
         s_rows = w_scales.rearrange("e a q n -> q (e a) n")
         for q in range(4):
             nc.sync.dma_start(
@@ -90,6 +90,11 @@ def tile_moe_two_lin_relu_kernel(tc, xT, w_words, w_scales, b, gate, offs, dst, 
         def scalar_copy(o, i):
             nc.scalar.activation(o, i, COPY)
 
+        def gather(dst_tile, window, s):
+            nc.vector.tensor_copy(
+                dst_tile[:, s : s + PIECE], window[:].indirect(offs_t[:, s // 16 : (s + PIECE) // 16])
+            )
+
         for a in range(PASSES):
             for c, (t0, w, v) in enumerate(CHUNKS[a]):
                 if v > 0:
@@ -100,10 +105,15 @@ def tile_moe_two_lin_relu_kernel(tc, xT, w_words, w_scales, b, gate, offs, dst, 
                     scales=planes[a][:, t0 : t0 + w],
                     in_=grouped[a, c][:].rearrange("p w j -> p (w j)"),
                 )
-            for s in range(0, SLOTS, PIECE):
-                lst = offs_t[:, s // 16 : (s + PIECE) // 16]
-                nc.vector.tensor_copy(g_codes[a][:, s : s + PIECE], codes[a][:].indirect(lst))
-                nc.vector.tensor_copy(g_planes[a][:, s : s + PIECE], planes[a][:].indirect(lst))
+            if a == 0:
+                gather(g_codes[0], codes[0], 0)
+                gather(g_codes[0], codes[0], PIECE)
+                gather(g_planes[0], planes[0], 0)
+            else:
+                gather(g_planes[0], planes[0], PIECE)
+                for s in range(0, SLOTS, PIECE):
+                    gather(g_codes[1], codes[1], s)
+                    gather(g_planes[1], planes[1], s)
 
         y = {}
         per = PIECE // C
@@ -132,12 +142,13 @@ def tile_moe_two_lin_relu_kernel(tc, xT, w_words, w_scales, b, gate, offs, dst, 
                     nc.scalar.activation(
                         y[h, s][:, i * C : (i + 1) * C], acc[h, i][:], RELU, bias=bias[:, h, e : e + 1]
                     )
-        for h in range(HALVES):
-            for s in range(0, SLOTS, PIECE):
+        for s in range(0, SLOTS, PIECE):
+            for h in range(HALVES):
                 nc.vector.tensor_tensor(
                     out_t[h][:].indirect(dst_t[:, s // 16 : (s + PIECE) // 16]),
                     y[h, s][:],
                     gate_t[h][:, s : s + PIECE],
                     MULT,
                 )
+        for h in range(HALVES):
             nc.sync.dma_start(out[h * P : (h + 1) * P, :], out_t[h][:])

from contextlib import ExitStack

import concourse.mybir as mybir

K, T, E, C, N = 1024, 1280, 8, 128, 256
SLOTS = E * C
FLOPS = 2 * K * SLOTS * N
P = 128
PACK = 4
PASSES = K // (P * PACK)
HALVES = N // P

F32 = mybir.dt.float32
BF16 = mybir.dt.bfloat16
I32 = mybir.dt.int32
U32 = mybir.dt.uint32
U16 = mybir.dt.uint16
U8 = mybir.dt.uint8
FP8X4 = mybir.dt.float8_e4m3fn_x4
FP4X4 = mybir.dt.float4_e2m1fn_x4
COPY = mybir.ActivationFunctionType.Copy
RELU = mybir.ActivationFunctionType.Relu
MULT = mybir.AluOpType.mult

CHUNKS = (
    ((0, 256, 160), (256, 512, 336), (768, 256, 192), (1024, 256, 192)),
    ((0, 512, 0), (512, 512, 64), (1024, 256, 128)),
)
PIECE = 512


def interleave(copy, grouped, raw, a, b):
    copy(
        grouped[:, a:b, :].rearrange("p (c i) t -> p c t i", i=4),
        raw[:, :, a:b].rearrange("p t (c i) -> p c t i", i=4),
    )


def tile_moe_two_lin_relu_kernel(tc, xT, w_words, w_scales, b, gate, offs, dst, out):
    nc = tc.nc
    with ExitStack() as ctx:
        keep = ctx.enter_context(tc.tile_pool(name="keep", bufs=1))
        psum = ctx.enter_context(tc.psum_pool(name="psum", bufs=1))

        offs_t = keep.tile([P, SLOTS // 16], U16, name="offs_t")
        dst_t = keep.tile([P, SLOTS // 16], U16, name="dst_t")
        ww = keep.tile([P, E * PASSES, 2 * N], U8, name="ww", align_bytes=64)
        ws = keep.tile([P, E * PASSES, N], U8, name="ws", align_bytes=64)
        gate_t = [keep.tile([P, SLOTS], F32, name=f"gate{h}") for h in range(HALVES)]
        bias = keep.tile([P, HALVES, E], F32, name="bias")
        out_t = [keep.tile([P, T], F32, name=f"out{h}") for h in range(HALVES)]
        codes = [keep.tile([P, T], U32, name=f"codes{a}", align_bytes=64) for a in range(PASSES)]
        planes = [keep.tile([P, T], U8, name=f"planes{a}", align_bytes=64) for a in range(PASSES)]
        g_codes = [keep.tile([P, SLOTS], U32, name=f"gcodes{a}", align_bytes=64) for a in range(PASSES)]
        g_planes = [keep.tile([P, SLOTS], U8, name=f"gplanes{a}", align_bytes=64) for a in range(PASSES)]
        raw = {}
        grouped = {}
        for a in range(PASSES):
            for c, (t0, w, v) in enumerate(CHUNKS[a]):
                raw[a, c] = keep.tile([P, PACK, w], F32, name=f"raw{a}_{c}")
                grouped[a, c] = keep.tile([P, w, PACK], BF16, name=f"grouped{a}_{c}", align_bytes=64)

        for a in range(PASSES):
            nc.gpsimd.memset(planes[a][:].bitcast(I32), 0)
        nc.gpsimd.memset(ws[:].rearrange("p x n -> p (x n)").bitcast(I32), 0)
        for h in range(HALVES):
            nc.gpsimd.memset(out_t[h][:], 0.0)

        x_rows = xT.rearrange("(a p j) t -> a p j t", p=P, j=PACK)
        for a in range(PASSES):
            for c, (t0, w, v) in enumerate(CHUNKS[a]):
                nc.sync.dma_start(raw[a, c][:], x_rows[a, :, :, t0 : t0 + w])
            if a == 0:
                nc.sync.dma_start(offs_t[:], offs)
        s_rows = w_scales.rearrange("e a q n -> q (e a) n")
        for q in range(4):
            nc.sync.dma_start(
                ws[32 * q : 32 * q + 4, :, :].bitcast(I32), s_rows[4 * q : 4 * q + 4, :, :].bitcast(I32)
            )
        w_rows = w_words.rearrange("e a p n -> p (e a) n")
        for part in range(2):
            x = slice(part * E * PASSES // 2, (part + 1) * E * PASSES // 2)
            nc.sync.dma_start(ww[:, x, :].bitcast(I32), w_rows[:, x, :].bitcast(I32))
            if part == 0:
                nc.sync.dma_start(bias[:], b.rearrange("(h p) e -> p h e", p=P))
                nc.sync.dma_start(dst_t[:], dst)
                nc.sync.dma_start(gate_t[0][:], gate[0:P, :])
        nc.sync.dma_start(gate_t[1][:], gate[P : 2 * P, :])

        def scalar_copy(o, i):
            nc.scalar.activation(o, i, COPY)

        def gather(dst_tile, window, s):
            nc.vector.tensor_copy(
                dst_tile[:, s : s + PIECE], window[:].indirect(offs_t[:, s // 16 : (s + PIECE) // 16])
            )

        for a in range(PASSES):
            for c, (t0, w, v) in enumerate(CHUNKS[a]):
                if v > 0:
                    interleave(nc.vector.tensor_copy, grouped[a, c], raw[a, c], 0, v)
                interleave(scalar_copy, grouped[a, c], raw[a, c], v, w)
                nc.vector.quantize_mx(
                    out=codes[a][:, t0 : t0 + w].bitcast(FP8X4),
                    scales=planes[a][:, t0 : t0 + w],
                    in_=grouped[a, c][:].rearrange("p w j -> p (w j)"),
                )
            if a == 0:
                gather(g_codes[0], codes[0], 0)
                gather(g_codes[0], codes[0], PIECE)
                gather(g_planes[0], planes[0], 0)
            else:
                gather(g_planes[0], planes[0], PIECE)
                for s in range(0, SLOTS, PIECE):
                    gather(g_codes[1], codes[1], s)
                    gather(g_planes[1], planes[1], s)

        y = {}
        per = PIECE // C
        for s in range(0, SLOTS, PIECE):
            acc = {}
            for a in range(PASSES):
                for h in range(HALVES):
                    for i in range(per):
                        if a == 0:
                            acc[h, i] = psum.tile([P, C], F32, name=f"acc{h}_{i}")
                        e = s // C + i
                        x = e * PASSES + a
                        nc.tensor.matmul_mx(
                            out=acc[h, i][:],
                            lhsT=ww[:, x, h * 2 * P : (h + 1) * 2 * P].bitcast(FP4X4),
                            lhsT_scale=ws[:, x, h * P : (h + 1) * P],
                            rhs=g_codes[a][:, e * C : (e + 1) * C].bitcast(FP8X4),
                            rhs_scale=g_planes[a][:, e * C : (e + 1) * C],
                            start=(a == 0),
                            stop=(a == PASSES - 1),
                        )
            for h in range(HALVES):
                y[h, s] = keep.tile([P, PIECE], F32, name=f"y{h}_{s}")
                for i in range(per):
                    e = s // C + i
                    nc.scalar.activation(
                        y[h, s][:, i * C : (i + 1) * C], acc[h, i][:], RELU, bias=bias[:, h, e : e + 1]
                    )
        for s in range(0, SLOTS, PIECE):
            for h in range(HALVES):
                nc.vector.tensor_tensor(
                    out_t[h][:].indirect(dst_t[:, s // 16 : (s + PIECE) // 16]),
                    y[h, s][:],
                    gate_t[h][:, s : s + PIECE],
                    MULT,
                )
        for h in range(HALVES):
            nc.sync.dma_start(out[h * P : (h + 1) * P, :], out_t[h][:])
